import numpy as np
import ml_dtypes


def mxq(x, axis, fmt="e4m3"):
    dtype, down = {"e4m3": (ml_dtypes.float8_e4m3fn, 7), "e5m2": (ml_dtypes.float8_e5m2, 14)}[fmt]
    v = np.moveaxis(np.asarray(x, np.float32).astype(ml_dtypes.bfloat16).astype(np.float64), axis, -1)
    blocks = v.reshape(v.shape[:-1] + (-1, 32))
    amax = np.abs(blocks).max(-1, keepdims=True)
    byte = np.maximum(np.where(amax > 0, np.frexp(amax)[1] - 1 + 127, 0) - down, 1)
    scale = np.exp2(byte - 127.0)
    codes = (blocks / scale).astype(np.float32).astype(dtype).astype(np.float64)
    return np.moveaxis((codes * scale).reshape(v.shape), -1, axis)


WIDE = False


def mx_kscale(k):
    if not WIDE:
        return np.ones(k)
    levels = np.array([10, -10, 5, -5, 0])
    if k % 512:
        return np.exp2(np.random.permutation(np.resize(levels, k // 32))).repeat(32)
    a = np.empty((k // 512, 16))
    for p in range(k // 512):
        a[p, :8] = np.random.permutation(np.resize(levels, 8))
        for g in range(8):
            far = levels[np.abs(levels - a[p, g]) >= 10]
            a[p, g + 8] = far[np.random.randint(len(far))]
    return np.exp2(a.ravel()).repeat(32)


BF16 = ml_dtypes.bfloat16


def bf(x):
    return np.asarray(x, np.float32).astype(BF16)


def f64(x):
    return np.asarray(x).astype(np.float64)


B, S, Z, E = 16, 512, 1024, 256


def sigmoid(x):
    return 1.0 / (1.0 + np.exp(-x))


def squared_relu(t):
    r = np.maximum(t, 0.0)
    return r * r


def draw0():
    s = mx_kscale(Z)
    r = mx_kscale(S)
    return {
        "z": bf(np.random.standard_normal((B, S, Z))),
        "gq": bf(np.random.standard_normal(Z) * s),
        "cq": bf(0.5 * np.random.standard_normal(Z) * s),
        "gk": bf(np.random.standard_normal(Z) / s),
        "g": bf(np.random.standard_normal(S) * r),
        "v": bf(0.25 * np.random.standard_normal((B, S, E)) / r[None, :, None]),
        "u": bf(np.random.standard_normal((B, S, E))),
    }


def core(z, gq, cq, gk, g, v, u):
    z, gq, cq, gk, g, v, u = f64(z), f64(gq), f64(cq), f64(gk), f64(g), f64(v), f64(u)
    width = z.shape[-1]
    q = z * gq[None, None, :] + cq[None, None, :]
    k = z * gk[None, None, :]
    t = (mxq(q, 2, "e4m3") @ mxq(k, 2, "e4m3").transpose(0, 2, 1)) / np.sqrt(width)
    a = squared_relu(t) / 8.0
    p = a * g[None, None, :]
    c = mxq(p, 2, "e4m3") @ mxq(v, 1, "e4m3")
    return u * sigmoid(u) * c


def e4m3fn_bytes(y):
    return np.clip(np.asarray(y, np.float64), -448.0, 448.0).astype(np.float32).astype(ml_dtypes.float8_e4m3fn).view(np.uint8)


def e4m3fn_values(b):
    return np.asarray(b, np.uint8).view(ml_dtypes.float8_e4m3fn).astype(np.float64)


def setup_inputs():
    d = draw0()
    x0 = np.asarray(d['v']).astype(np.float64)
    s = (np.max(np.abs(x0), axis=(0, 2), keepdims=True) / 448.0).astype(np.float32)
    out = {}
    for k, v in d.items():
        if k == 'v':
            out['v_bytes'] = e4m3fn_bytes(x0 / s.astype(np.float64))
            out['v_scale'] = s
        else:
            out[k] = v
    return out


def reference(z, gq, cq, gk, g, v_bytes, v_scale, u):
    return core(z, gq, cq, gk, g, e4m3fn_values(v_bytes) * v_scale.astype(np.float64), u)

@@ -1,0 +1,316 @@
+from contextlib import ExitStack
+
+import concourse.mybir as mybir
+from concourse.masks import make_identity
+
+B, S, Z, E = 16, 512, 1024, 256
+FLOPS = 2 * B * S * S * (Z + E)
+
+F32 = mybir.dt.float32
+BF16 = mybir.dt.bfloat16
+U32 = mybir.dt.uint32
+U8 = mybir.dt.uint8
+FP8 = mybir.dt.float8_e4m3fn
+FP8X4 = mybir.dt.float8_e4m3fn_x4
+ALU = mybir.AluOpType
+ACT = mybir.ActivationFunctionType
+
+P = 128
+PACK = 4
+PASSES = Z // (P * PACK)
+HALF = S // 2
+Z_BUFS, K_BUFS = 3, 3
+GP_COLS = 448
+GP_COLS_FIRST = 192
+GP_COLS_LAST = 256
+
+
+def tile_gatedattentionunitsquaredrelu_t_kernel(tc, z, gq, cq, gk, g, v_bytes, v_scale, u, out):
+    nc = tc.nc
+    with ExitStack() as ctx:
+        sb = ctx.enter_context(tc.tile_pool(name="sb", bufs=1))
+        ps = ctx.enter_context(tc.psum_pool(name="ps", bufs=1))
+
+        def tiles(name, count, shape, dtype, pool=sb):
+            if pool is sb:
+                return [pool.tile(shape, dtype, name="%s%d" % (name, i), align_bytes=64) for i in range(count)]
+            return [pool.tile(shape, dtype, name="%s%d" % (name, i)) for i in range(count)]
+
+        ident = tiles("ident", 1, [P, P], F32)[0]
+        gq_raw, cq_raw, gk_sb = tiles("gain", 3, [P, PASSES, PACK], BF16)
+        gq_sb, cq_sb = tiles("gain32", 2, [P, PASSES, PACK], F32)
+        g_raw = tiles("g_raw", 1, [P, PACK], BF16)[0]
+        vs_raw, g_sign, g_abs, half, root0, root_inv, root_fix, g_root, vs_signed = tiles("small", 9, [P, PACK], F32)
+
+        z_sb = tiles("z_sb", 2 * Z_BUFS, [P, 2, Z], BF16)
+        u_sb = tiles("u_sb", 2, [P, PACK * E], BF16)
+        vb_sb = tiles("vb_sb", 2, [P, PACK * E], U8)
+        k_il = tiles("k_il", 1, [P, PASSES * S * PACK], BF16)[0]
+        q_pl = tiles("q_pl", 2, [P, PASSES * PACK * S], BF16)
+        q_il = tiles("q_il", 1, [P, PASSES * S * PACK], BF16)[0]
+        k_codes = tiles("k_codes", K_BUFS, [P, PASSES * S], U32)
+        k_scales = tiles("k_scales", K_BUFS, [P, PASSES * S], U8)
+        q_codes = tiles("q_codes", 2, [P, PASSES * S], U32)
+        q_scales = tiles("q_scales", 2, [P, PASSES * S], U8)
+        r_sb = tiles("r_sb", 2, [P, 2 * P * PACK], F32)
+        p_il = tiles("p_il", 1, [P, S * PACK], BF16)[0]
+        p_codes = tiles("p_codes", 2, [P, S], U32)
+        p_scales = tiles("p_scales", 2, [P, S], U8)
+        v_pl = tiles("v_pl", 1, [P, PACK * E], BF16)[0]
+        v_il = tiles("v_il", 1, [P, E * PACK], BF16)[0]
+        v_codes = tiles("v_codes", 2, [P, E], U32)
+        v_scales = tiles("v_scales", 2, [P, E], U8)
+        gate = tiles("gate", 2, [P, PACK * E], F32)
+        o_sb = tiles("o_sb", 2, [P, PACK * E], F32)
+
+        z_bank = tiles("z_bank", 4, [P, 2 * HALF], F32, ps)
+        s_bank = tiles("s_bank", 2, [P, PACK * P], F32, ps)
+        c_bank = tiles("c_bank", 2, [P, 2 * E], F32, ps)
+
+        def live(b):
+            return 0 <= b < B
+
+        def load_z(b):
+            if live(b):
+                rows = z[b].rearrange("(m t) c -> m t c", t=PACK)
+                for h in range(2):
+                    nc.sync.dma_start(out=z_sb[2 * (b % Z_BUFS) + h][:], in_=rows[:, 2 * h : 2 * h + 2, :])
+
+        def load_u(b):
+            if live(b):
+                nc.sync.dma_start(out=u_sb[b % 2][:], in_=u[b].rearrange("(m t) e -> m (t e)", t=PACK))
+
+        def load_v(b):
+            if live(b):
+                nc.sync.dma_start(out=vb_sb[b % 2][:], in_=v_bytes[b].rearrange("(m t) e -> m (t e)", t=PACK))
+
+        def load_constants():
+            for dst, src in ((gk_sb, gk), (gq_raw, gq), (cq_raw, cq)):
+                nc.scalar.dma_start(out=dst[:], in_=src.rearrange("(g p t) -> p g t", p=P, t=PACK))
+            nc.scalar.dma_start(out=g_raw[:], in_=g.rearrange("(p t) -> p t", t=PACK))
+            nc.scalar.dma_start(out=vs_raw[:], in_=v_scale.rearrange("o (p t) x -> p (o t x)", t=PACK))
+
+        def widen_gains():
+            nc.vector.tensor_copy(out=gq_sb[:], in_=gq_raw[:])
+            nc.vector.tensor_copy(out=cq_sb[:], in_=cq_raw[:])
+
+        def key_gain_first():
+            nc.vector.memset(half[:], 0.5)
+            nc.vector.tensor_scalar(out=g_sign[:], in0=g_raw[:], scalar1=0.0, scalar2=2.0, op0=ALU.is_ge, op1=ALU.mult)
+            nc.vector.tensor_scalar(out=g_sign[:], in0=g_sign[:], scalar1=-1.0, scalar2=None, op0=ALU.add)
+            nc.vector.scalar_tensor_tensor(
+                out=g_abs[:], in0=g_raw[:], scalar=1.0 / (Z * 8.0), in1=g_sign[:], op0=ALU.mult, op1=ALU.mult
+            )
+            nc.vector.tensor_tensor(out=vs_signed[:], in0=vs_raw[:], in1=g_sign[:], op=ALU.mult)
+            nc.gpsimd.tensor_tensor(out=root0[:], in0=g_abs[:], in1=half[:], op=ALU.pow)
+
+        def key_gain_second():
+            nc.vector.tensor_scalar(out=root_inv[:], in0=root0[:], scalar1=2.0**-80, scalar2=None, op0=ALU.max)
+            nc.vector.reciprocal(out=root_inv[:], in_=root_inv[:])
+            nc.vector.scalar_tensor_tensor(
+                out=root_fix[:], in0=g_abs[:], scalar=0.5, in1=root_inv[:], op0=ALU.mult, op1=ALU.mult
+            )
+            nc.vector.scalar_tensor_tensor(
+                out=g_root[:], in0=root0[:], scalar=0.5, in1=root_fix[:], op0=ALU.mult, op1=ALU.add
+            )
+
+        def turn(b, i):
+            if live(b):
+                h, gp = divmod(i, PASSES)
+                src = z_sb[2 * (b % Z_BUFS) + h]
+                for w in range(2):
+                    for slot in range(2):
+                        words = src[:, slot, :].bitcast(F32)
+                        col = w * HALF + slot * P
+                        nc.tensor.transpose(
+                            z_bank[i][:, col : col + P], words[:, 256 * gp + w : 256 * (gp + 1) : 2], ident[:]
+                        )
+
+        def bank_view(i):
+            return z_bank[i][:].bitcast(BF16).rearrange("p (w n e) -> p n w e", w=2, e=2)
+
+        def make_k(b, i):
+            if live(b):
+                h, gp = divmod(i, PASSES)
+                at = (gp * S + h * HALF) * PACK
+                dst = k_il[:, at : at + HALF * PACK].rearrange("p (n w e) -> p n w e", w=2, e=2)
+                gain = gk_sb[:, gp, :].rearrange("p (o w e) -> p o w e", o=1, w=2).to_broadcast([P, HALF, 2, 2])
+                nc.vector.tensor_tensor(out=dst, in0=bank_view(i), in1=gain, op=ALU.mult)
+
+        def make_q(b, i):
+            if live(b):
+                h, gp = divmod(i, PASSES)
+                for t in range(PACK):
+                    at = (gp * PACK + t) * S + h * HALF
+                    nc.scalar.activation(
+                        out=q_pl[b % 2][:, at : at + HALF],
+                        in_=bank_view(i)[:, :, t // 2, t % 2],
+                        func=ACT.Identity,
+                        scale=gq_sb[:, gp, t : t + 1],
+                        bias=cq_sb[:, gp, t : t + 1],
+                    )
+
+        def gp_cols(b):
+            return GP_COLS_FIRST if b == 0 else GP_COLS_LAST if b == B - 1 else GP_COLS
+
+        def weave_q_gpsimd(b):
+            if live(b) and gp_cols(b) > 0:
+                n = gp_cols(b)
+                src = q_pl[b % 2][:].rearrange("p (g t n) -> p g n t", g=PASSES, t=PACK)[:, :, :n, :]
+                dst = q_il[:].rearrange("p (g n t) -> p g n t", g=PASSES, t=PACK)[:, :, :n, :]
+                nc.gpsimd.tensor_scalar(out=dst, in0=src, scalar1=1.0, scalar2=0.0, op0=ALU.mult, op1=ALU.add)
+
+        def weave_q_vector(b):
+            if live(b):
+                c0 = gp_cols(b) // 4
+                src = q_pl[b % 2][:].rearrange("p (g t c i) -> p g c t i", g=PASSES, t=PACK, i=4)[:, :, c0:, :, :]
+                dst = q_il[:].rearrange("p (g c i t) -> p g c t i", g=PASSES, t=PACK, i=4)[:, :, c0:, :, :]
+                nc.vector.tensor_copy(out=dst, in_=src)
+
+        def quantize(codes, scales, src):
+            nc.vector.quantize_mx(out=codes[:].bitcast(FP8X4), scales=scales[:], in_=src[:])
+
+        def quant_k(b):
+            if live(b):
+                quantize(k_codes[b % K_BUFS], k_scales[b % K_BUFS], k_il)
+
+        def quant_q(b):
+            if live(b):
+                quantize(q_codes[b % 2], q_scales[b % 2], q_il)
+
+        def quant_p(b):
+            if live(b):
+                quantize(p_codes[b % 2], p_scales[b % 2], p_il)
+
+        def quant_v(b):
+            if live(b):
+                quantize(v_codes[b % 2], v_scales[b % 2], v_il)
+
+        def scores(b, tq):
+            if live(b):
+                for tk in range(PACK):
+                    for gp in range(PASSES):
+                        kc = slice(gp * S + tk * P, gp * S + (tk + 1) * P)
+                        qc = slice(gp * S + tq * P, gp * S + (tq + 1) * P)
+                        nc.tensor.matmul_mx(
+                            out=s_bank[tq % 2][:, tk * P : (tk + 1) * P],
+                            lhsT=k_codes[b % K_BUFS][:, kc].bitcast(FP8X4),
+                            lhsT_scale=k_scales[b % K_BUFS][:, kc],
+                            rhs=q_codes[b % 2][:, qc].bitcast(FP8X4),
+                            rhs_scale=q_scales[b % 2][:, qc],
+                            start=(gp == 0),
+                            stop=(gp == PASSES - 1),
+                        )
+
+        def relu_root(b, tq):
+            if live(b):
+                root = g_root[:].rearrange("p (o t) -> p o t", o=1).to_broadcast([P, P, PACK])
+                nc.vector.scalar_tensor_tensor(
+                    out=r_sb[tq // 2][:, (tq % 2) * S : (tq % 2 + 1) * S].rearrange("p (n t) -> p n t", t=PACK),
+                    in0=s_bank[tq % 2][:].rearrange("p (t n) -> p n t", t=PACK),
+                    scalar=0.0,
+                    in1=root,
+                    op0=ALU.max,
+                    op1=ALU.mult,
+                )
+
+        def square(b, h):
+            if live(b):
+                nc.scalar.activation(out=p_il[:, h * 2 * S : (h + 1) * 2 * S], in_=r_sb[h][:], func=ACT.Square)
+
+        def widen_v(b):
+            if live(b):
+                for t in range(PACK):
+                    cols = slice(t * E, (t + 1) * E)
+                    nc.scalar.activation(
+                        out=v_pl[:, cols], in_=vb_sb[b % 2][:, cols].bitcast(FP8), func=ACT.Copy, scale=vs_signed[:, t : t + 1]
+                    )
+
+        def weave_v(b):
+            if live(b):
+                src = v_pl[:].rearrange("p (t c i) -> p c t i", t=PACK, i=4)
+                dst = v_il[:].rearrange("p (c i t) -> p c t i", t=PACK, i=4)
+                nc.vector.tensor_copy(out=dst, in_=src)
+
+        def silu(b):
+            if live(b):
+                nc.scalar.activation(out=gate[b % 2][:], in_=u_sb[b % 2][:], func=ACT.Silu)
+
+        def mix(b):
+            if live(b):
+                for tq in range(PACK):
+                    cols = slice(tq * P, (tq + 1) * P)
+                    nc.tensor.matmul_mx(
+                        out=c_bank[tq // 2][:, (tq % 2) * E : (tq % 2 + 1) * E],
+                        lhsT=p_codes[b % 2][:, cols].bitcast(FP8X4),
+                        lhsT_scale=p_scales[b % 2][:, cols],
+                        rhs=v_codes[b % 2][:].bitcast(FP8X4),
+                        rhs_scale=v_scales[b % 2][:],
+                        start=True,
+                        stop=True,
+                    )
+
+        def finish(b, h):
+            if live(b):
+                cols = slice(h * 2 * E, (h + 1) * 2 * E)
+                nc.vector.tensor_tensor(out=o_sb[b % 2][:, cols], in0=c_bank[h][:], in1=gate[b % 2][:, cols], op=ALU.mult)
+
+        def store(b):
+            if live(b):
+                nc.sync.dma_start(out=out[b].rearrange("(m t) e -> m (t e)", t=PACK), in_=o_sb[b % 2][:])
+
+        ctx.enter_context(tc.manual_schedule())
+        load_z(0)
+        load_constants()
+        make_identity(nc, ident[:])
+        widen_gains()
+        load_u(0)
+        load_z(1)
+        silu(0)
+        for i in range(4):
+            turn(0, i)
+        for n in range(-2, B + 1):
+            weave_q_gpsimd(n + 1)
+            load_z(n + 4)
+            load_v(n + 1)
+            if n >= 1:
+                load_u(n)
+            scores(n, 0)
+            scores(n, 1)
+            make_q(n + 2, 0)
+            make_k(n + 2, 1)
+            make_k(n + 2, 2)
+            make_k(n + 2, 3)
+            relu_root(n, 0)
+            scores(n, 2)
+            make_q(n + 2, 1)
+            make_k(n + 2, 0)
+            turn(n + 3, 1)
+            turn(n + 3, 0)
+            relu_root(n, 1)
+            scores(n, 3)
+            make_q(n + 2, 2)
+            turn(n + 3, 2)
+            finish(n - 1, 0)
+            relu_root(n, 2)
+            finish(n - 1, 1)
+            store(n - 1)
+            relu_root(n, 3)
+            square(n, 0)
+            make_q(n + 2, 3)
+            turn(n + 3, 3)
+            square(n, 1)
+            if n == -2:
+                key_gain_first()
+            quant_k(n + 2)
+            weave_v(n)
+            weave_q_vector(n + 1)
+            if n == -1:
+                key_gain_second()
+            quant_v(n)
+            quant_p(n)
+            mix(n)
+            quant_q(n + 1)
+            widen_v(n + 1)
+            if n >= 1:
+                silu(n)

@@ -20,9 +20,6 @@ PACK = 4
 PASSES = Z // (P * PACK)
 HALF = S // 2
 Z_BUFS, K_BUFS = 3, 3
-GP_COLS = 448
-GP_COLS_FIRST = 192
-GP_COLS_LAST = 256
 
 
 def tile_gatedattentionunitsquaredrelu_t_kernel(tc, z, gq, cq, gk, g, v_bytes, v_scale, u, out):
@@ -40,12 +37,12 @@ def tile_gatedattentionunitsquaredrelu_t_kernel(tc, z, gq, cq, gk, g, v_bytes, v
         gq_raw, cq_raw, gk_sb = tiles("gain", 3, [P, PASSES, PACK], BF16)
         gq_sb, cq_sb = tiles("gain32", 2, [P, PASSES, PACK], F32)
         g_raw = tiles("g_raw", 1, [P, PACK], BF16)[0]
-        vs_raw, g_sign, g_abs, half, root0, root_inv, root_fix, g_root, vs_signed = tiles("small", 9, [P, PACK], F32)
+        vs_raw, g_neg, g_sign, g_unit, g_abs, half, root0, root_inv, root_fix, g_root, vs_signed = tiles("small", 11, [P, PACK], F32)
 
-        z_sb = tiles("z_sb", 2 * Z_BUFS, [P, 2, Z], BF16)
+        z_sb = tiles("z_sb", 4 * Z_BUFS, [P, 2, Z // PASSES], BF16)
         u_sb = tiles("u_sb", 2, [P, PACK * E], BF16)
         vb_sb = tiles("vb_sb", 2, [P, PACK * E], U8)
-        k_il = tiles("k_il", 1, [P, PASSES * S * PACK], BF16)[0]
+        k_il = tiles("k_il", 2, [P, PASSES * S * PACK], BF16)
         q_pl = tiles("q_pl", 2, [P, PASSES * PACK * S], BF16)
         q_il = tiles("q_il", 1, [P, PASSES * S * PACK], BF16)[0]
         k_codes = tiles("k_codes", K_BUFS, [P, PASSES * S], U32)
@@ -63,18 +60,32 @@ def tile_gatedattentionunitsquaredrelu_t_kernel(tc, z, gq, cq, gk, g, v_bytes, v
         gate = tiles("gate", 2, [P, PACK * E], F32)
         o_sb = tiles("o_sb", 2, [P, PACK * E], F32)
 
-        z_bank = tiles("z_bank", 4, [P, 2 * HALF], F32, ps)
-        s_bank = tiles("s_bank", 2, [P, PACK * P], F32, ps)
-        c_bank = tiles("c_bank", 2, [P, 2 * E], F32, ps)
+        banks = tiles("bank", 8, [P, 2 * HALF], F32, ps)
+
+        def s_bank(b, tq):
+            if b >= B - 2 and tq >= 2:
+                return banks[2 * (b - (B - 2)) + tq - 2]
+            return banks[4 + tq % 2]
+
+        def c_place(b, tq):
+            if b == B - 1:
+                return banks[tq if tq < 2 else tq + 2][:, :E]
+            return banks[6 + tq // 2][:, (tq % 2) * E : (tq % 2 + 1) * E]
+
+        def z_bank(b, i):
+            return banks[4 + i] if b == 1 else banks[i]
 
         def live(b):
             return 0 <= b < B
 
-        def load_z(b):
+        def load_z(b, parts=range(4)):
             if live(b):
                 rows = z[b].rearrange("(m t) c -> m t c", t=PACK)
-                for h in range(2):
-                    nc.sync.dma_start(out=z_sb[2 * (b % Z_BUFS) + h][:], in_=rows[:, 2 * h : 2 * h + 2, :])
+                for i in parts:
+                    h, gp = divmod(i, PASSES)
+                    nc.sync.dma_start(
+                        out=z_sb[4 * (b % Z_BUFS) + i][:], in_=rows[:, 2 * h : 2 * h + 2, 512 * gp : 512 * (gp + 1)]
+                    )
 
         def load_u(b):
             if live(b):
@@ -85,115 +96,107 @@ def tile_gatedattentionunitsquaredrelu_t_kernel(tc, z, gq, cq, gk, g, v_bytes, v
                 nc.sync.dma_start(out=vb_sb[b % 2][:], in_=v_bytes[b].rearrange("(m t) e -> m (t e)", t=PACK))
 
         def load_constants():
-            for dst, src in ((gk_sb, gk), (gq_raw, gq), (cq_raw, cq)):
+            for dst, src in ((gq_raw, gq), (cq_raw, cq), (gk_sb, gk)):
                 nc.scalar.dma_start(out=dst[:], in_=src.rearrange("(g p t) -> p g t", p=P, t=PACK))
             nc.scalar.dma_start(out=g_raw[:], in_=g.rearrange("(p t) -> p t", t=PACK))
-            nc.scalar.dma_start(out=vs_raw[:], in_=v_scale.rearrange("o (p t) x -> p (o t x)", t=PACK))
 
         def widen_gains():
             nc.vector.tensor_copy(out=gq_sb[:], in_=gq_raw[:])
             nc.vector.tensor_copy(out=cq_sb[:], in_=cq_raw[:])
 
-        def key_gain_first():
-            nc.vector.memset(half[:], 0.5)
-            nc.vector.tensor_scalar(out=g_sign[:], in0=g_raw[:], scalar1=0.0, scalar2=2.0, op0=ALU.is_ge, op1=ALU.mult)
-            nc.vector.tensor_scalar(out=g_sign[:], in0=g_sign[:], scalar1=-1.0, scalar2=None, op0=ALU.add)
-            nc.vector.scalar_tensor_tensor(
-                out=g_abs[:], in0=g_raw[:], scalar=1.0 / (Z * 8.0), in1=g_sign[:], op0=ALU.mult, op1=ALU.mult
+        def split_key_gain():
+            nc.gpsimd.tensor_scalar(out=g_neg[:], in0=g_raw[:], scalar1=0.0, scalar2=-2.0, op0=ALU.is_lt, op1=ALU.mult)
+            nc.gpsimd.tensor_scalar(
+                out=g_unit[:], in0=g_neg[:], scalar1=1.0, scalar2=1.0 / (Z * 8.0), op0=ALU.add, op1=ALU.mult
             )
-            nc.vector.tensor_tensor(out=vs_signed[:], in0=vs_raw[:], in1=g_sign[:], op=ALU.mult)
-            nc.gpsimd.tensor_tensor(out=root0[:], in0=g_abs[:], in1=half[:], op=ALU.pow)
+            nc.gpsimd.tensor_tensor(out=g_abs[:], in0=g_raw[:], in1=g_unit[:], op=ALU.mult)
+            nc.gpsimd.tensor_scalar(out=g_sign[:], in0=g_neg[:], scalar1=1.0, scalar2=1.0, op0=ALU.add, op1=ALU.mult)
+            nc.gpsimd.tensor_tensor(out=vs_signed[:], in0=vs_raw[:], in1=g_sign[:], op=ALU.mult)
 
-        def key_gain_second():
-            nc.vector.tensor_scalar(out=root_inv[:], in0=root0[:], scalar1=2.0**-80, scalar2=None, op0=ALU.max)
-            nc.vector.reciprocal(out=root_inv[:], in_=root_inv[:])
-            nc.vector.scalar_tensor_tensor(
-                out=root_fix[:], in0=g_abs[:], scalar=0.5, in1=root_inv[:], op0=ALU.mult, op1=ALU.mult
-            )
-            nc.vector.scalar_tensor_tensor(
-                out=g_root[:], in0=root0[:], scalar=0.5, in1=root_fix[:], op0=ALU.mult, op1=ALU.add
-            )
+        def polish_root(step):
+            if step == 0:
+                nc.vector.tensor_scalar(out=root_inv[:], in0=root0[:], scalar1=2.0**-80, scalar2=None, op0=ALU.max)
+            elif step == 1:
+                nc.vector.reciprocal(out=root_inv[:], in_=root_inv[:])
+            elif step == 2:
+                nc.vector.scalar_tensor_tensor(
+                    out=root_fix[:], in0=g_abs[:], scalar=0.5, in1=root_inv[:], op0=ALU.mult, op1=ALU.mult
+                )
+            else:
+                nc.vector.scalar_tensor_tensor(
+                    out=g_root[:], in0=root0[:], scalar=0.5, in1=root_fix[:], op0=ALU.mult, op1=ALU.add
+                )
 
         def turn(b, i):
             if live(b):
-                h, gp = divmod(i, PASSES)
-                src = z_sb[2 * (b % Z_BUFS) + h]
+                src = z_sb[4 * (b % Z_BUFS) + i]
                 for w in range(2):
                     for slot in range(2):
                         words = src[:, slot, :].bitcast(F32)
                         col = w * HALF + slot * P
-                        nc.tensor.transpose(
-                            z_bank[i][:, col : col + P], words[:, 256 * gp + w : 256 * (gp + 1) : 2], ident[:]
-                        )
+                        nc.tensor.transpose(z_bank(b, i)[:, col : col + P], words[:, w::2], ident[:])
 
-        def bank_view(i):
-            return z_bank[i][:].bitcast(BF16).rearrange("p (w n e) -> p n w e", w=2, e=2)
+        def bank_view(b, i):
+            return z_bank(b, i)[:].bitcast(BF16).rearrange("p (w n e) -> p n w e", w=2, e=2)
 
         def make_k(b, i):
             if live(b):
-                h, gp = divmod(i, PASSES)
-                at = (gp * S + h * HALF) * PACK
-                dst = k_il[:, at : at + HALF * PACK].rearrange("p (n w e) -> p n w e", w=2, e=2)
+                gp = i % PASSES
+                at = i * HALF * PACK
+                dst = k_il[b % 2][:, at : at + HALF * PACK].rearrange("p (n w e) -> p n w e", w=2, e=2)
                 gain = gk_sb[:, gp, :].rearrange("p (o w e) -> p o w e", o=1, w=2).to_broadcast([P, HALF, 2, 2])
-                nc.vector.tensor_tensor(out=dst, in0=bank_view(i), in1=gain, op=ALU.mult)
+                nc.vector.tensor_tensor(out=dst, in0=bank_view(b, i), in1=gain, op=ALU.mult)
 
         def make_q(b, i):
             if live(b):
-                h, gp = divmod(i, PASSES)
+                gp = i % PASSES
                 for t in range(PACK):
-                    at = (gp * PACK + t) * S + h * HALF
-                    nc.scalar.activation(
-                        out=q_pl[b % 2][:, at : at + HALF],
-                        in_=bank_view(i)[:, :, t // 2, t % 2],
-                        func=ACT.Identity,
-                        scale=gq_sb[:, gp, t : t + 1],
-                        bias=cq_sb[:, gp, t : t + 1],
-                    )
+                    at = (i * PACK + t) * HALF
+                    dst, src = q_pl[b % 2][:, at : at + HALF], bank_view(b, i)[:, :, t // 2, t % 2]
+                    gain, offset = gq_sb[:, gp, t : t + 1], cq_sb[:, gp, t : t + 1]
+                    nc.scalar.activation(out=dst, in_=src, func=ACT.Identity, scale=gain, bias=offset)
 
-        def gp_cols(b):
-            return GP_COLS_FIRST if b == 0 else GP_COLS_LAST if b == B - 1 else GP_COLS
-
-        def weave_q_gpsimd(b):
-            if live(b) and gp_cols(b) > 0:
-                n = gp_cols(b)
-                src = q_pl[b % 2][:].rearrange("p (g t n) -> p g n t", g=PASSES, t=PACK)[:, :, :n, :]
-                dst = q_il[:].rearrange("p (g n t) -> p g n t", g=PASSES, t=PACK)[:, :, :n, :]
+        def weave_q_gpsimd(b, i0=0, i1=4):
+            if live(b):
+                src = q_pl[b % 2][:].rearrange("p (i t n) -> p i n t", i=4, t=PACK)[:, i0:i1, :, :]
+                dst = q_il[:].rearrange("p (i n t) -> p i n t", i=4, t=PACK)[:, i0:i1, :, :]
                 nc.gpsimd.tensor_scalar(out=dst, in0=src, scalar1=1.0, scalar2=0.0, op0=ALU.mult, op1=ALU.add)
 
-        def weave_q_vector(b):
-            if live(b):
-                c0 = gp_cols(b) // 4
-                src = q_pl[b % 2][:].rearrange("p (g t c i) -> p g c t i", g=PASSES, t=PACK, i=4)[:, :, c0:, :, :]
-                dst = q_il[:].rearrange("p (g c i t) -> p g c t i", g=PASSES, t=PACK, i=4)[:, :, c0:, :, :]
-                nc.vector.tensor_copy(out=dst, in_=src)
+        def weave_q_views(b, i0, i1):
+            src = q_pl[b % 2][:].rearrange("p (i t c j) -> p i c t j", i=4, t=PACK, j=4)[:, i0:i1, :, :, :]
+            dst = q_il[:].rearrange("p (i c j t) -> p i c t j", i=4, t=PACK, j=4)[:, i0:i1, :, :, :]
+            return dst, src
 
         def quantize(codes, scales, src):
             nc.vector.quantize_mx(out=codes[:].bitcast(FP8X4), scales=scales[:], in_=src[:])
 
         def quant_k(b):
             if live(b):
-                quantize(k_codes[b % K_BUFS], k_scales[b % K_BUFS], k_il)
+                quantize(k_codes[b % K_BUFS], k_scales[b % K_BUFS], k_il[b % 2])
 
         def quant_q(b):
             if live(b):
                 quantize(q_codes[b % 2], q_scales[b % 2], q_il)
 
-        def quant_p(b):
-            if live(b):
-                quantize(p_codes[b % 2], p_scales[b % 2], p_il)
+        def quant_p(b, t0=0, t1=PACK):
+            cols = slice(t0 * P, t1 * P)
+            quantize(p_codes[b % 2][:, cols], p_scales[b % 2][:, cols], p_il[:, t0 * S : t1 * S])
 
         def quant_v(b):
             if live(b):
                 quantize(v_codes[b % 2], v_scales[b % 2], v_il)
 
+        def code_cols(slot, gp):
+            at = ((slot // 2) * PASSES + gp) * HALF + (slot % 2) * P
+            return slice(at, at + P)
+
         def scores(b, tq):
             if live(b):
                 for tk in range(PACK):
                     for gp in range(PASSES):
-                        kc = slice(gp * S + tk * P, gp * S + (tk + 1) * P)
-                        qc = slice(gp * S + tq * P, gp * S + (tq + 1) * P)
+                        kc, qc = code_cols(tk, gp), code_cols(tq, gp)
                         nc.tensor.matmul_mx(
-                            out=s_bank[tq % 2][:, tk * P : (tk + 1) * P],
+                            out=s_bank(b, tq)[:, tk * P : (tk + 1) * P],
                             lhsT=k_codes[b % K_BUFS][:, kc].bitcast(FP8X4),
                             lhsT_scale=k_scales[b % K_BUFS][:, kc],
                             rhs=q_codes[b % 2][:, qc].bitcast(FP8X4),
@@ -207,7 +210,7 @@ def tile_gatedattentionunitsquaredrelu_t_kernel(tc, z, gq, cq, gk, g, v_bytes, v
                 root = g_root[:].rearrange("p (o t) -> p o t", o=1).to_broadcast([P, P, PACK])
                 nc.vector.scalar_tensor_tensor(
                     out=r_sb[tq // 2][:, (tq % 2) * S : (tq % 2 + 1) * S].rearrange("p (n t) -> p n t", t=PACK),
-                    in0=s_bank[tq % 2][:].rearrange("p (t n) -> p n t", t=PACK),
+                    in0=s_bank(b, tq)[:].rearrange("p (t n) -> p n t", t=PACK),
                     scalar=0.0,
                     in1=root,
                     op0=ALU.max,
@@ -218,6 +221,10 @@ def tile_gatedattentionunitsquaredrelu_t_kernel(tc, z, gq, cq, gk, g, v_bytes, v
             if live(b):
                 nc.scalar.activation(out=p_il[:, h * 2 * S : (h + 1) * 2 * S], in_=r_sb[h][:], func=ACT.Square)
 
+        def square_slot(tq):
+            src = r_sb[tq // 2][:, (tq % 2) * S : (tq % 2 + 1) * S]
+            nc.scalar.activation(out=p_il[:, tq * S : (tq + 1) * S], in_=src, func=ACT.Square)
+
         def widen_v(b):
             if live(b):
                 for t in range(PACK):
@@ -226,22 +233,26 @@ def tile_gatedattentionunitsquaredrelu_t_kernel(tc, z, gq, cq, gk, g, v_bytes, v
                         out=v_pl[:, cols], in_=vb_sb[b % 2][:, cols].bitcast(FP8), func=ACT.Copy, scale=vs_signed[:, t : t + 1]
                     )
 
-        def weave_v(b):
-            if live(b):
-                src = v_pl[:].rearrange("p (t c i) -> p c t i", t=PACK, i=4)
-                dst = v_il[:].rearrange("p (c i t) -> p c t i", t=PACK, i=4)
-                nc.vector.tensor_copy(out=dst, in_=src)
+        def weave_v():
+            src = v_pl[:].rearrange("p (t c i) -> p c t i", t=PACK, i=4)
+            dst = v_il[:].rearrange("p (c i t) -> p c t i", t=PACK, i=4)
+            nc.vector.tensor_copy(out=dst, in_=src)
+
+        def weave_v_gpsimd():
+            src = v_pl[:].rearrange("p (t e) -> p e t", t=PACK)
+            dst = v_il[:].rearrange("p (e t) -> p e t", t=PACK)
+            nc.gpsimd.tensor_scalar(out=dst, in0=src, scalar1=1.0, scalar2=0.0, op0=ALU.mult, op1=ALU.add)
 
         def silu(b):
             if live(b):
                 nc.scalar.activation(out=gate[b % 2][:], in_=u_sb[b % 2][:], func=ACT.Silu)
 
-        def mix(b):
+        def mix(b, slots=range(PACK)):
             if live(b):
-                for tq in range(PACK):
+                for tq in slots:
                     cols = slice(tq * P, (tq + 1) * P)
                     nc.tensor.matmul_mx(
-                        out=c_bank[tq // 2][:, (tq % 2) * E : (tq % 2 + 1) * E],
+                        out=c_place(b, tq),
                         lhsT=p_codes[b % 2][:, cols].bitcast(FP8X4),
                         lhsT_scale=p_scales[b % 2][:, cols],
                         rhs=v_codes[b % 2][:].bitcast(FP8X4),
@@ -253,64 +264,154 @@ def tile_gatedattentionunitsquaredrelu_t_kernel(tc, z, gq, cq, gk, g, v_bytes, v
         def finish(b, h):
             if live(b):
                 cols = slice(h * 2 * E, (h + 1) * 2 * E)
-                nc.vector.tensor_tensor(out=o_sb[b % 2][:, cols], in0=c_bank[h][:], in1=gate[b % 2][:, cols], op=ALU.mult)
+                nc.vector.tensor_tensor(out=o_sb[b % 2][:, cols], in0=banks[6 + h][:], in1=gate[b % 2][:, cols], op=ALU.mult)
 
-        def store(b):
+        def finish_slot(b, tq):
+            cols = slice(tq * E, (tq + 1) * E)
+            nc.vector.tensor_tensor(out=o_sb[b % 2][:, cols], in0=c_place(b, tq), in1=gate[b % 2][:, cols], op=ALU.mult)
+
+        def store(b, h0=0, h1=2):
             if live(b):
-                nc.sync.dma_start(out=out[b].rearrange("(m t) e -> m (t e)", t=PACK), in_=o_sb[b % 2][:])
+                cols = slice(h0 * 2 * E, h1 * 2 * E)
+                nc.sync.dma_start(out=out[b].rearrange("(m t) e -> m (t e)", t=PACK)[:, cols], in_=o_sb[b % 2][:, cols])
 
         ctx.enter_context(tc.manual_schedule())
-        load_z(0)
+        load_z(0, range(2))
         load_constants()
+        load_u(0)
+        load_z(0, range(2, 4))
+        nc.sync.dma_start(out=vs_raw[:], in_=v_scale.rearrange("o (p t) x -> p (o t x)", t=PACK))
+        load_z(1)
+        load_v(0)
+        load_z(2)
         make_identity(nc, ident[:])
         widen_gains()
-        load_u(0)
-        load_z(1)
+        split_key_gain()
         silu(0)
-        for i in range(4):
-            turn(0, i)
-        for n in range(-2, B + 1):
+        for b in range(2):
+            for i in range(4):
+                turn(b, i)
+        make_q(0, 0)
+        make_k(0, 1)
+        make_q(0, 1)
+        make_k(0, 2)
+        make_k(0, 0)
+        make_q(0, 2)
+        make_k(0, 3)
+        nc.vector.memset(half[:], 0.5)
+        quant_k(0)
+        nc.gpsimd.tensor_tensor(out=root0[:], in0=g_abs[:], in1=half[:], op=ALU.pow)
+        weave_q_gpsimd(0, 0, 1)
+        make_q(0, 3)
+        for i in range(3):
+            turn(2, i)
+        load_z(3)
+        make_q(1, 0)
+        for i in (1, 2, 3, 0):
+            make_k(1, i)
+        for i in range(1, 4):
+            make_q(1, i)
+        for step, (i0, i1) in enumerate(((1, 2), (2, 4))):
+            dst, src = weave_q_views(0, i0, i1)
+            nc.vector.tensor_copy(out=dst, in_=src)
+            polish_root(step)
+        widen_v(0)
+        quant_q(0)
+        polish_root(2)
+        scores(0, 0)
+        scores(0, 1)
+        turn(2, 3)
+        quant_k(1)
+        polish_root(3)
+
+        for n in range(B - 2):
             weave_q_gpsimd(n + 1)
             load_z(n + 4)
             load_v(n + 1)
-            if n >= 1:
-                load_u(n)
-            scores(n, 0)
-            scores(n, 1)
+            load_u(n + 1)
             make_q(n + 2, 0)
             make_k(n + 2, 1)
-            make_k(n + 2, 2)
-            make_k(n + 2, 3)
             relu_root(n, 0)
             scores(n, 2)
             make_q(n + 2, 1)
-            make_k(n + 2, 0)
-            turn(n + 3, 1)
-            turn(n + 3, 0)
+            make_k(n + 2, 2)
             relu_root(n, 1)
             scores(n, 3)
+            turn(n + 3, 1)
+            square(n, 0)
+            make_k(n + 2, 3)
+            relu_root(n, 2)
+            make_k(n + 2, 0)
+            turn(n + 3, 0)
+            relu_root(n, 3)
             make_q(n + 2, 2)
             turn(n + 3, 2)
+            square(n, 1)
             finish(n - 1, 0)
-            relu_root(n, 2)
             finish(n - 1, 1)
             store(n - 1)
-            relu_root(n, 3)
-            square(n, 0)
             make_q(n + 2, 3)
-            turn(n + 3, 3)
-            square(n, 1)
-            if n == -2:
-                key_gain_first()
-            quant_k(n + 2)
-            weave_v(n)
-            weave_q_vector(n + 1)
-            if n == -1:
-                key_gain_second()
-            quant_v(n)
+            weave_v()
             quant_p(n)
+            quant_v(n)
             mix(n)
             quant_q(n + 1)
+            scores(n + 1, 0)
+            scores(n + 1, 1)
+            turn(n + 3, 3)
+            quant_k(n + 2)
             widen_v(n + 1)
             if n >= 1:
                 silu(n)
+
+        n = B - 2
+        weave_q_gpsimd(n + 1, 0, 2)
+        load_v(n + 1)
+        load_u(n + 1)
+        scores(n, 2)
+        scores(n, 3)
+        dst, src = weave_q_views(n + 1, 2, 4)
+        nc.scalar.copy(out=dst, in_=src)
+        relu_root(n, 0)
+        relu_root(n, 1)
+        square(n, 0)
+        relu_root(n, 2)
+        relu_root(n, 3)
+        square(n, 1)
+        finish(n - 1, 0)
+        finish(n - 1, 1)
+        store(n - 1)
+        quant_q(n + 1)
+        for tq in range(PACK):
+            scores(n + 1, tq)
+        weave_v()
+        silu(n)
+        widen_v(n + 1)
+        silu(n + 1)
+        quant_p(n)
+        quant_v(n)
+        mix(n)
+        weave_v_gpsimd()
+
+        n = B - 1
+        relu_root(n, 0)
+        relu_root(n, 1)
+        square(n, 0)
+        relu_root(n, 2)
+        square_slot(2)
+        relu_root(n, 3)
+        square_slot(3)
+        finish(n - 1, 0)
+        quant_v(n)
+        quant_p(n, 0, 2)
+        mix(n, range(2))
+        finish(n - 1, 1)
+        store(n - 1)
+        quant_p(n, 2, 4)
+        mix(n, range(2, 4))
+        finish_slot(n, 0)
+        finish_slot(n, 1)
+        store(n, 0, 1)
+        finish_slot(n, 2)
+        finish_slot(n, 3)
+        store(n, 1, 2)

@@ -20,6 +20,9 @@ PACK = 4
 PASSES = Z // (P * PACK)
 HALF = S // 2
 Z_BUFS, K_BUFS = 3, 3
+COLS = PASSES * S
+GP_COLS = 960
+GP_COLS_FIRST = 896
 
 
 def tile_gatedattentionunitsquaredrelu_t_kernel(tc, z, gq, cq, gk, g, v_bytes, v_scale, u, out):
@@ -34,6 +37,7 @@ def tile_gatedattentionunitsquaredrelu_t_kernel(tc, z, gq, cq, gk, g, v_bytes, v
             return [pool.tile(shape, dtype, name="%s%d" % (name, i)) for i in range(count)]
 
         ident = tiles("ident", 1, [P, P], F32)[0]
+        ident16 = tiles("ident16", 1, [P, P], BF16)[0]
         gq_raw, cq_raw, gk_sb = tiles("gain", 3, [P, PASSES, PACK], BF16)
         gq_sb, cq_sb = tiles("gain32", 2, [P, PASSES, PACK], F32)
         g_raw = tiles("g_raw", 1, [P, PACK], BF16)[0]
@@ -42,9 +46,8 @@ def tile_gatedattentionunitsquaredrelu_t_kernel(tc, z, gq, cq, gk, g, v_bytes, v
         z_sb = tiles("z_sb", 4 * Z_BUFS, [P, 2, Z // PASSES], BF16)
         u_sb = tiles("u_sb", 2, [P, PACK * E], BF16)
         vb_sb = tiles("vb_sb", 2, [P, PACK * E], U8)
-        k_il = tiles("k_il", 2, [P, PASSES * S * PACK], BF16)
+        woven = tiles("woven", 2, [P, PASSES * S * PACK], BF16)
         q_pl = tiles("q_pl", 2, [P, PASSES * PACK * S], BF16)
-        q_il = tiles("q_il", 1, [P, PASSES * S * PACK], BF16)[0]
         k_codes = tiles("k_codes", K_BUFS, [P, PASSES * S], U32)
         k_scales = tiles("k_scales", K_BUFS, [P, PASSES * S], U8)
         q_codes = tiles("q_codes", 2, [P, PASSES * S], U32)
@@ -53,7 +56,7 @@ def tile_gatedattentionunitsquaredrelu_t_kernel(tc, z, gq, cq, gk, g, v_bytes, v
         p_il = tiles("p_il", 1, [P, S * PACK], BF16)[0]
         p_codes = tiles("p_codes", 2, [P, S], U32)
         p_scales = tiles("p_scales", 2, [P, S], U8)
-        v_pl = tiles("v_pl", 1, [P, PACK * E], BF16)[0]
+        v_pl = tiles("v_pl", 2, [P, PACK * E], BF16)
         v_il = tiles("v_il", 1, [P, E * PACK], BF16)[0]
         v_codes = tiles("v_codes", 2, [P, E], U32)
         v_scales = tiles("v_scales", 2, [P, E], U8)
@@ -110,6 +113,7 @@ def tile_gatedattentionunitsquaredrelu_t_kernel(tc, z, gq, cq, gk, g, v_bytes, v
                 out=g_unit[:], in0=g_neg[:], scalar1=1.0, scalar2=1.0 / (Z * 8.0), op0=ALU.add, op1=ALU.mult
             )
             nc.gpsimd.tensor_tensor(out=g_abs[:], in0=g_raw[:], in1=g_unit[:], op=ALU.mult)
+            nc.gpsimd.tensor_tensor(out=root0[:], in0=g_abs[:], in1=half[:], op=ALU.pow)
             nc.gpsimd.tensor_scalar(out=g_sign[:], in0=g_neg[:], scalar1=1.0, scalar2=1.0, op0=ALU.add, op1=ALU.mult)
             nc.gpsimd.tensor_tensor(out=vs_signed[:], in0=vs_raw[:], in1=g_sign[:], op=ALU.mult)
 
@@ -143,7 +147,7 @@ def tile_gatedattentionunitsquaredrelu_t_kernel(tc, z, gq, cq, gk, g, v_bytes, v
             if live(b):
                 gp = i % PASSES
                 at = i * HALF * PACK
-                dst = k_il[b % 2][:, at : at + HALF * PACK].rearrange("p (n w e) -> p n w e", w=2, e=2)
+                dst = woven[b % 2][:, at : at + HALF * PACK].rearrange("p (n w e) -> p n w e", w=2, e=2)
                 gain = gk_sb[:, gp, :].rearrange("p (o w e) -> p o w e", o=1, w=2).to_broadcast([P, HALF, 2, 2])
                 nc.vector.tensor_tensor(out=dst, in0=bank_view(b, i), in1=gain, op=ALU.mult)
 
@@ -151,20 +155,19 @@ def tile_gatedattentionunitsquaredrelu_t_kernel(tc, z, gq, cq, gk, g, v_bytes, v
             if live(b):
                 gp = i % PASSES
                 for t in range(PACK):
-                    at = (i * PACK + t) * HALF
+                    at = t * COLS + i * HALF
                     dst, src = q_pl[b % 2][:, at : at + HALF], bank_view(b, i)[:, :, t // 2, t % 2]
                     gain, offset = gq_sb[:, gp, t : t + 1], cq_sb[:, gp, t : t + 1]
                     nc.scalar.activation(out=dst, in_=src, func=ACT.Identity, scale=gain, bias=offset)
 
-        def weave_q_gpsimd(b, i0=0, i1=4):
-            if live(b):
-                src = q_pl[b % 2][:].rearrange("p (i t n) -> p i n t", i=4, t=PACK)[:, i0:i1, :, :]
-                dst = q_il[:].rearrange("p (i n t) -> p i n t", i=4, t=PACK)[:, i0:i1, :, :]
-                nc.gpsimd.tensor_scalar(out=dst, in0=src, scalar1=1.0, scalar2=0.0, op0=ALU.mult, op1=ALU.add)
+        def weave_q_gpsimd(b, c0, c1):
+            src = q_pl[b % 2][:].rearrange("p (t n) -> p n t", t=PACK)[:, c0:c1, :]
+            dst = woven[b % 2][:].rearrange("p (n t) -> p n t", t=PACK)[:, c0:c1, :]
+            nc.gpsimd.tensor_scalar(out=dst, in0=src, scalar1=1.0, scalar2=0.0, op0=ALU.mult, op1=ALU.add)
 
-        def weave_q_views(b, i0, i1):
-            src = q_pl[b % 2][:].rearrange("p (i t c j) -> p i c t j", i=4, t=PACK, j=4)[:, i0:i1, :, :, :]
-            dst = q_il[:].rearrange("p (i c j t) -> p i c t j", i=4, t=PACK, j=4)[:, i0:i1, :, :, :]
+        def weave_q_views(b, c0, c1):
+            src = q_pl[b % 2][:].rearrange("p (t m j) -> p m t j", t=PACK, j=4)[:, c0 // 4 : c1 // 4, :, :]
+            dst = woven[b % 2][:].rearrange("p (m j t) -> p m t j", t=PACK, j=4)[:, c0 // 4 : c1 // 4, :, :]
             return dst, src
 
         def quantize(codes, scales, src):
@@ -172,11 +175,10 @@ def tile_gatedattentionunitsquaredrelu_t_kernel(tc, z, gq, cq, gk, g, v_bytes, v
 
         def quant_k(b):
             if live(b):
-                quantize(k_codes[b % K_BUFS], k_scales[b % K_BUFS], k_il[b % 2])
+                quantize(k_codes[b % K_BUFS], k_scales[b % K_BUFS], woven[b % 2])
 
-        def quant_q(b):
-            if live(b):
-                quantize(q_codes[b % 2], q_scales[b % 2], q_il)
+        def quant_q(b, c0=0, c1=COLS):
+            quantize(q_codes[b % 2][:, c0:c1], q_scales[b % 2][:, c0:c1], woven[b % 2][:, c0 * PACK : c1 * PACK])
 
         def quant_p(b, t0=0, t1=PACK):
             cols = slice(t0 * P, t1 * P)
@@ -225,23 +227,23 @@ def tile_gatedattentionunitsquaredrelu_t_kernel(tc, z, gq, cq, gk, g, v_bytes, v
             src = r_sb[tq // 2][:, (tq % 2) * S : (tq % 2 + 1) * S]
             nc.scalar.activation(out=p_il[:, tq * S : (tq + 1) * S], in_=src, func=ACT.Square)
 
-        def widen_v(b):
-            if live(b):
-                for t in range(PACK):
-                    cols = slice(t * E, (t + 1) * E)
-                    nc.scalar.activation(
-                        out=v_pl[:, cols], in_=vb_sb[b % 2][:, cols].bitcast(FP8), func=ACT.Copy, scale=vs_signed[:, t : t + 1]
-                    )
+        def widen_v(b, on_scalar=False):
+            for t in range(PACK):
+                cols = slice(t * E, (t + 1) * E)
+                dst, src, scale = v_pl[b % 2][:, cols], vb_sb[b % 2][:, cols].bitcast(FP8), vs_signed[:, t : t + 1]
+                if on_scalar:
+                    nc.scalar.activation(out=dst, in_=src, func=ACT.Copy, scale=scale)
+                else:
+                    nc.vector.tensor_scalar(out=dst, in0=src, scalar1=scale, scalar2=None, op0=ALU.mult)
 
-        def weave_v():
-            src = v_pl[:].rearrange("p (t c i) -> p c t i", t=PACK, i=4)
-            dst = v_il[:].rearrange("p (c i t) -> p c t i", t=PACK, i=4)
-            nc.vector.tensor_copy(out=dst, in_=src)
+        def weave_v(b, bank):
+            src = v_pl[b % 2][:].rearrange("p (t e) -> p e t", t=PACK)
+            for h in range(2):
+                dst = bank[:].bitcast(BF16)[:, h * S : (h + 1) * S].rearrange("p (e t) -> p e t", t=PACK)
+                nc.tensor.matmul(out=dst, lhsT=ident16[:], rhs=src[:, h * P : (h + 1) * P, :], start=True, stop=True)
 
-        def weave_v_gpsimd():
-            src = v_pl[:].rearrange("p (t e) -> p e t", t=PACK)
-            dst = v_il[:].rearrange("p (e t) -> p e t", t=PACK)
-            nc.gpsimd.tensor_scalar(out=dst, in0=src, scalar1=1.0, scalar2=0.0, op0=ALU.mult, op1=ALU.add)
+        def fetch_v(bank):
+            nc.scalar.copy(out=v_il[:], in_=bank[:].bitcast(BF16))
 
         def silu(b):
             if live(b):
@@ -276,15 +278,17 @@ def tile_gatedattentionunitsquaredrelu_t_kernel(tc, z, gq, cq, gk, g, v_bytes, v
                 nc.sync.dma_start(out=out[b].rearrange("(m t) e -> m (t e)", t=PACK)[:, cols], in_=o_sb[b % 2][:, cols])
 
         ctx.enter_context(tc.manual_schedule())
-        load_z(0, range(2))
-        load_constants()
+        load_z(0, range(1))
         load_u(0)
-        load_z(0, range(2, 4))
+        load_constants()
+        load_z(0, range(1, 4))
         nc.sync.dma_start(out=vs_raw[:], in_=v_scale.rearrange("o (p t) x -> p (o t x)", t=PACK))
         load_z(1)
         load_v(0)
         load_z(2)
         make_identity(nc, ident[:])
+        nc.vector.tensor_copy(out=ident16[:], in_=ident[:])
+        nc.gpsimd.memset(half[:], 0.5)
         widen_gains()
         split_key_gain()
         silu(0)
@@ -298,12 +302,10 @@ def tile_gatedattentionunitsquaredrelu_t_kernel(tc, z, gq, cq, gk, g, v_bytes, v
         make_k(0, 0)
         make_q(0, 2)
         make_k(0, 3)
-        nc.vector.memset(half[:], 0.5)
         quant_k(0)
-        nc.gpsimd.tensor_tensor(out=root0[:], in0=g_abs[:], in1=half[:], op=ALU.pow)
-        weave_q_gpsimd(0, 0, 1)
         make_q(0, 3)
-        for i in range(3):
+        weave_q_gpsimd(0, 0, HALF)
+        for i in range(4):
             turn(2, i)
         load_z(3)
         make_q(1, 0)
@@ -311,29 +313,33 @@ def tile_gatedattentionunitsquaredrelu_t_kernel(tc, z, gq, cq, gk, g, v_bytes, v
             make_k(1, i)
         for i in range(1, 4):
             make_q(1, i)
-        for step, (i0, i1) in enumerate(((1, 2), (2, 4))):
-            dst, src = weave_q_views(0, i0, i1)
-            nc.vector.tensor_copy(out=dst, in_=src)
-            polish_root(step)
-        widen_v(0)
+        polish_root(0)
+        dst, src = weave_q_views(0, HALF, COLS)
+        nc.vector.tensor_copy(out=dst, in_=src)
+        polish_root(1)
+        widen_v(0, on_scalar=True)
         quant_q(0)
         polish_root(2)
         scores(0, 0)
         scores(0, 1)
-        turn(2, 3)
         quant_k(1)
         polish_root(3)
 
         for n in range(B - 2):
-            weave_q_gpsimd(n + 1)
+            split = GP_COLS if n >= 1 else GP_COLS_FIRST
+            weave_q_gpsimd(n + 1, 0, split)
             load_z(n + 4)
             load_v(n + 1)
             load_u(n + 1)
+            dst, src = weave_q_views(n + 1, split, COLS)
+            nc.scalar.copy(out=dst, in_=src)
+            make_k(n + 2, 0)
             make_q(n + 2, 0)
             make_k(n + 2, 1)
+            make_q(n + 2, 1)
             relu_root(n, 0)
             scores(n, 2)
-            make_q(n + 2, 1)
+            turn(n + 3, 0)
             make_k(n + 2, 2)
             relu_root(n, 1)
             scores(n, 3)
@@ -341,69 +347,71 @@ def tile_gatedattentionunitsquaredrelu_t_kernel(tc, z, gq, cq, gk, g, v_bytes, v
             square(n, 0)
             make_k(n + 2, 3)
             relu_root(n, 2)
-            make_k(n + 2, 0)
-            turn(n + 3, 0)
+            finish(n - 1, 0)
+            weave_v(n, banks[6])
             relu_root(n, 3)
+            finish(n - 1, 1)
+            store(n - 1)
             make_q(n + 2, 2)
             turn(n + 3, 2)
             square(n, 1)
-            finish(n - 1, 0)
-            finish(n - 1, 1)
-            store(n - 1)
+            fetch_v(banks[6])
             make_q(n + 2, 3)
-            weave_v()
-            quant_p(n)
-            quant_v(n)
-            mix(n)
+            widen_v(n + 1)
             quant_q(n + 1)
             scores(n + 1, 0)
             scores(n + 1, 1)
             turn(n + 3, 3)
+            quant_p(n)
             quant_k(n + 2)
-            widen_v(n + 1)
+            quant_v(n)
+            mix(n)
             if n >= 1:
                 silu(n)
 
         n = B - 2
-        weave_q_gpsimd(n + 1, 0, 2)
+        weave_q_gpsimd(n + 1, 0, S)
         load_v(n + 1)
         load_u(n + 1)
         scores(n, 2)
         scores(n, 3)
-        dst, src = weave_q_views(n + 1, 2, 4)
+        dst, src = weave_q_views(n + 1, S, S + HALF)
         nc.scalar.copy(out=dst, in_=src)
         relu_root(n, 0)
         relu_root(n, 1)
         square(n, 0)
+        finish(n - 1, 0)
+        weave_v(n, banks[6])
         relu_root(n, 2)
         relu_root(n, 3)
         square(n, 1)
-        finish(n - 1, 0)
+        fetch_v(banks[6])
         finish(n - 1, 1)
         store(n - 1)
-        quant_q(n + 1)
-        for tq in range(PACK):
-            scores(n + 1, tq)
-        weave_v()
-        silu(n)
+        quant_q(n + 1, 0, S)
+        scores(n + 1, 0)
+        scores(n + 1, 1)
+        dst, src = weave_q_views(n + 1, S + HALF, COLS)
+        nc.vector.tensor_copy(out=dst, in_=src)
         widen_v(n + 1)
-        silu(n + 1)
+        weave_v(n + 1, banks[0])
+        quant_q(n + 1, S, COLS)
+        scores(n + 1, 2)
+        scores(n + 1, 3)
+        silu(n)
         quant_p(n)
         quant_v(n)
         mix(n)
-        weave_v_gpsimd()
+        silu(n + 1)
+        fetch_v(banks[0])
 
         n = B - 1
-        relu_root(n, 0)
-        relu_root(n, 1)
-        square(n, 0)
-        relu_root(n, 2)
-        square_slot(2)
-        relu_root(n, 3)
-        square_slot(3)
+        for tq in range(PACK):
+            relu_root(n, tq)
+            square_slot(tq)
         finish(n - 1, 0)
-        quant_v(n)
         quant_p(n, 0, 2)
+        quant_v(n)
         mix(n, range(2))
         finish(n - 1, 1)
         store(n - 1)

@@ -21,8 +21,10 @@ PASSES = Z // (P * PACK)
 HALF = S // 2
 Z_BUFS, K_BUFS = 3, 3
 COLS = PASSES * S
-GP_COLS = 960
+GP_COLS = 992
+SC_PLANES = 1
 GP_COLS_FIRST = 896
+GP_COLS_LAST = 512
 
 
 def tile_gatedattentionunitsquaredrelu_t_kernel(tc, z, gq, cq, gk, g, v_bytes, v_scale, u, out):
@@ -227,8 +229,8 @@ def tile_gatedattentionunitsquaredrelu_t_kernel(tc, z, gq, cq, gk, g, v_bytes, v
             src = r_sb[tq // 2][:, (tq % 2) * S : (tq % 2 + 1) * S]
             nc.scalar.activation(out=p_il[:, tq * S : (tq + 1) * S], in_=src, func=ACT.Square)
 
-        def widen_v(b, on_scalar=False):
-            for t in range(PACK):
+        def widen_v(b, planes=range(PACK), on_scalar=False):
+            for t in planes:
                 cols = slice(t * E, (t + 1) * E)
                 dst, src, scale = v_pl[b % 2][:, cols], vb_sb[b % 2][:, cols].bitcast(FP8), vs_signed[:, t : t + 1]
                 if on_scalar:
@@ -304,19 +306,19 @@ def tile_gatedattentionunitsquaredrelu_t_kernel(tc, z, gq, cq, gk, g, v_bytes, v
         make_k(0, 3)
         quant_k(0)
         make_q(0, 3)
-        weave_q_gpsimd(0, 0, HALF)
         for i in range(4):
             turn(2, i)
         load_z(3)
         make_q(1, 0)
-        for i in (1, 2, 3, 0):
-            make_k(1, i)
-        for i in range(1, 4):
-            make_q(1, i)
-        polish_root(0)
-        dst, src = weave_q_views(0, HALF, COLS)
-        nc.vector.tensor_copy(out=dst, in_=src)
-        polish_root(1)
+        for h in range(2):
+            make_k(1, h + 1)
+            make_q(1, h + 1)
+            dst, src = weave_q_views(0, h * S, (h + 1) * S)
+            nc.vector.tensor_copy(out=dst, in_=src)
+            polish_root(h)
+        make_k(1, 3)
+        make_q(1, 3)
+        make_k(1, 0)
         widen_v(0, on_scalar=True)
         quant_q(0)
         polish_root(2)
@@ -357,7 +359,7 @@ def tile_gatedattentionunitsquaredrelu_t_kernel(tc, z, gq, cq, gk, g, v_bytes, v
             square(n, 1)
             fetch_v(banks[6])
             make_q(n + 2, 3)
-            widen_v(n + 1)
+            widen_v(n + 1, range(SC_PLANES, PACK))
             quant_q(n + 1)
             scores(n + 1, 0)
             scores(n + 1, 1)
@@ -366,16 +368,17 @@ def tile_gatedattentionunitsquaredrelu_t_kernel(tc, z, gq, cq, gk, g, v_bytes, v
             quant_k(n + 2)
             quant_v(n)
             mix(n)
+            widen_v(n + 1, range(SC_PLANES), on_scalar=True)
             if n >= 1:
                 silu(n)
 
         n = B - 2
-        weave_q_gpsimd(n + 1, 0, S)
+        weave_q_gpsimd(n + 1, 0, GP_COLS_LAST)
         load_v(n + 1)
         load_u(n + 1)
         scores(n, 2)
         scores(n, 3)
-        dst, src = weave_q_views(n + 1, S, S + HALF)
+        dst, src = weave_q_views(n + 1, GP_COLS_LAST, COLS)
         nc.scalar.copy(out=dst, in_=src)
         relu_root(n, 0)
         relu_root(n, 1)
@@ -391,8 +394,6 @@ def tile_gatedattentionunitsquaredrelu_t_kernel(tc, z, gq, cq, gk, g, v_bytes, v
         quant_q(n + 1, 0, S)
         scores(n + 1, 0)
         scores(n + 1, 1)
-        dst, src = weave_q_views(n + 1, S + HALF, COLS)
-        nc.vector.tensor_copy(out=dst, in_=src)
         widen_v(n + 1)
         weave_v(n + 1, banks[0])
         quant_q(n + 1, S, COLS)
@@ -402,13 +403,13 @@ def tile_gatedattentionunitsquaredrelu_t_kernel(tc, z, gq, cq, gk, g, v_bytes, v
         quant_p(n)
         quant_v(n)
         mix(n)
-        silu(n + 1)
         fetch_v(banks[0])
 
         n = B - 1
         for tq in range(PACK):
             relu_root(n, tq)
             square_slot(tq)
+        silu(n)
         finish(n - 1, 0)
         quant_p(n, 0, 2)
         quant_v(n)

from contextlib import ExitStack

import concourse.mybir as mybir
from concourse.masks import make_identity

B, S, Z, E = 16, 512, 1024, 256
FLOPS = 2 * B * S * S * (Z + E)

F32 = mybir.dt.float32
BF16 = mybir.dt.bfloat16
U32 = mybir.dt.uint32
U8 = mybir.dt.uint8
FP8 = mybir.dt.float8_e4m3fn
FP8X4 = mybir.dt.float8_e4m3fn_x4
ALU = mybir.AluOpType
ACT = mybir.ActivationFunctionType

P = 128
PACK = 4
PASSES = Z // (P * PACK)
HALF = S // 2
Z_BUFS, K_BUFS = 3, 3
COLS = PASSES * S
GP_COLS = 992
SC_PLANES = 1
GP_COLS_FIRST = 896
GP_COLS_LAST = 512


def tile_gatedattentionunitsquaredrelu_t_kernel(tc, z, gq, cq, gk, g, v_bytes, v_scale, u, out):
    nc = tc.nc
    with ExitStack() as ctx:
        sb = ctx.enter_context(tc.tile_pool(name="sb", bufs=1))
        ps = ctx.enter_context(tc.psum_pool(name="ps", bufs=1))

        def tiles(name, count, shape, dtype, pool=sb):
            if pool is sb:
                return [pool.tile(shape, dtype, name="%s%d" % (name, i), align_bytes=64) for i in range(count)]
            return [pool.tile(shape, dtype, name="%s%d" % (name, i)) for i in range(count)]

        ident = tiles("ident", 1, [P, P], F32)[0]
        ident16 = tiles("ident16", 1, [P, P], BF16)[0]
        gq_raw, cq_raw, gk_sb = tiles("gain", 3, [P, PASSES, PACK], BF16)
        gq_sb, cq_sb = tiles("gain32", 2, [P, PASSES, PACK], F32)
        g_raw = tiles("g_raw", 1, [P, PACK], BF16)[0]
        vs_raw, g_neg, g_sign, g_unit, g_abs, half, root0, root_inv, root_fix, g_root, vs_signed = tiles("small", 11, [P, PACK], F32)

        z_sb = tiles("z_sb", 4 * Z_BUFS, [P, 2, Z // PASSES], BF16)
        u_sb = tiles("u_sb", 2, [P, PACK * E], BF16)
        vb_sb = tiles("vb_sb", 2, [P, PACK * E], U8)
        woven = tiles("woven", 2, [P, PASSES * S * PACK], BF16)
        q_pl = tiles("q_pl", 2, [P, PASSES * PACK * S], BF16)
        k_codes = tiles("k_codes", K_BUFS, [P, PASSES * S], U32)
        k_scales = tiles("k_scales", K_BUFS, [P, PASSES * S], U8)
        q_codes = tiles("q_codes", 2, [P, PASSES * S], U32)
        q_scales = tiles("q_scales", 2, [P, PASSES * S], U8)
        r_sb = tiles("r_sb", 2, [P, 2 * P * PACK], F32)
        p_il = tiles("p_il", 1, [P, S * PACK], BF16)[0]
        p_codes = tiles("p_codes", 2, [P, S], U32)
        p_scales = tiles("p_scales", 2, [P, S], U8)
        v_pl = tiles("v_pl", 2, [P, PACK * E], BF16)
        v_il = tiles("v_il", 1, [P, E * PACK], BF16)[0]
        v_codes = tiles("v_codes", 2, [P, E], U32)
        v_scales = tiles("v_scales", 2, [P, E], U8)
        gate = tiles("gate", 2, [P, PACK * E], F32)
        o_sb = tiles("o_sb", 2, [P, PACK * E], F32)

        banks = tiles("bank", 8, [P, 2 * HALF], F32, ps)

        def s_bank(b, tq):
            if b >= B - 2 and tq >= 2:
                return banks[2 * (b - (B - 2)) + tq - 2]
            return banks[4 + tq % 2]

        def c_place(b, tq):
            if b == B - 1:
                return banks[tq if tq < 2 else tq + 2][:, :E]
            return banks[6 + tq // 2][:, (tq % 2) * E : (tq % 2 + 1) * E]

        def z_bank(b, i):
            return banks[4 + i] if b == 1 else banks[i]

        def live(b):
            return 0 <= b < B

        def load_z(b, parts=range(4)):
            if live(b):
                rows = z[b].rearrange("(m t) c -> m t c", t=PACK)
                for i in parts:
                    h, gp = divmod(i, PASSES)
                    nc.sync.dma_start(
                        out=z_sb[4 * (b % Z_BUFS) + i][:], in_=rows[:, 2 * h : 2 * h + 2, 512 * gp : 512 * (gp + 1)]
                    )

        def load_u(b):
            if live(b):
                nc.sync.dma_start(out=u_sb[b % 2][:], in_=u[b].rearrange("(m t) e -> m (t e)", t=PACK))

        def load_v(b):
            if live(b):
                nc.sync.dma_start(out=vb_sb[b % 2][:], in_=v_bytes[b].rearrange("(m t) e -> m (t e)", t=PACK))

        def load_constants():
            for dst, src in ((gq_raw, gq), (cq_raw, cq), (gk_sb, gk)):
                nc.scalar.dma_start(out=dst[:], in_=src.rearrange("(g p t) -> p g t", p=P, t=PACK))
            nc.scalar.dma_start(out=g_raw[:], in_=g.rearrange("(p t) -> p t", t=PACK))

        def widen_gains():
            nc.vector.tensor_copy(out=gq_sb[:], in_=gq_raw[:])
            nc.vector.tensor_copy(out=cq_sb[:], in_=cq_raw[:])

        def split_key_gain():
            nc.gpsimd.tensor_scalar(out=g_neg[:], in0=g_raw[:], scalar1=0.0, scalar2=-2.0, op0=ALU.is_lt, op1=ALU.mult)
            nc.gpsimd.tensor_scalar(
                out=g_unit[:], in0=g_neg[:], scalar1=1.0, scalar2=1.0 / (Z * 8.0), op0=ALU.add, op1=ALU.mult
            )
            nc.gpsimd.tensor_tensor(out=g_abs[:], in0=g_raw[:], in1=g_unit[:], op=ALU.mult)
            nc.gpsimd.tensor_tensor(out=root0[:], in0=g_abs[:], in1=half[:], op=ALU.pow)
            nc.gpsimd.tensor_scalar(out=g_sign[:], in0=g_neg[:], scalar1=1.0, scalar2=1.0, op0=ALU.add, op1=ALU.mult)
            nc.gpsimd.tensor_tensor(out=vs_signed[:], in0=vs_raw[:], in1=g_sign[:], op=ALU.mult)

        def polish_root(step):
            if step == 0:
                nc.vector.tensor_scalar(out=root_inv[:], in0=root0[:], scalar1=2.0**-80, scalar2=None, op0=ALU.max)
            elif step == 1:
                nc.vector.reciprocal(out=root_inv[:], in_=root_inv[:])
            elif step == 2:
                nc.vector.scalar_tensor_tensor(
                    out=root_fix[:], in0=g_abs[:], scalar=0.5, in1=root_inv[:], op0=ALU.mult, op1=ALU.mult
                )
            else:
                nc.vector.scalar_tensor_tensor(
                    out=g_root[:], in0=root0[:], scalar=0.5, in1=root_fix[:], op0=ALU.mult, op1=ALU.add
                )

        def turn(b, i):
            if live(b):
                src = z_sb[4 * (b % Z_BUFS) + i]
                for w in range(2):
                    for slot in range(2):
                        words = src[:, slot, :].bitcast(F32)
                        col = w * HALF + slot * P
                        nc.tensor.transpose(z_bank(b, i)[:, col : col + P], words[:, w::2], ident[:])

        def bank_view(b, i):
            return z_bank(b, i)[:].bitcast(BF16).rearrange("p (w n e) -> p n w e", w=2, e=2)

        def make_k(b, i):
            if live(b):
                gp = i % PASSES
                at = i * HALF * PACK
                dst = woven[b % 2][:, at : at + HALF * PACK].rearrange("p (n w e) -> p n w e", w=2, e=2)
                gain = gk_sb[:, gp, :].rearrange("p (o w e) -> p o w e", o=1, w=2).to_broadcast([P, HALF, 2, 2])
                nc.vector.tensor_tensor(out=dst, in0=bank_view(b, i), in1=gain, op=ALU.mult)

        def make_q(b, i):
            if live(b):
                gp = i % PASSES
                for t in range(PACK):
                    at = t * COLS + i * HALF
                    dst, src = q_pl[b % 2][:, at : at + HALF], bank_view(b, i)[:, :, t // 2, t % 2]
                    gain, offset = gq_sb[:, gp, t : t + 1], cq_sb[:, gp, t : t + 1]
                    nc.scalar.activation(out=dst, in_=src, func=ACT.Identity, scale=gain, bias=offset)

        def weave_q_gpsimd(b, c0, c1):
            src = q_pl[b % 2][:].rearrange("p (t n) -> p n t", t=PACK)[:, c0:c1, :]
            dst = woven[b % 2][:].rearrange("p (n t) -> p n t", t=PACK)[:, c0:c1, :]
            nc.gpsimd.tensor_scalar(out=dst, in0=src, scalar1=1.0, scalar2=0.0, op0=ALU.mult, op1=ALU.add)

        def weave_q_views(b, c0, c1):
            src = q_pl[b % 2][:].rearrange("p (t m j) -> p m t j", t=PACK, j=4)[:, c0 // 4 : c1 // 4, :, :]
            dst = woven[b % 2][:].rearrange("p (m j t) -> p m t j", t=PACK, j=4)[:, c0 // 4 : c1 // 4, :, :]
            return dst, src

        def quantize(codes, scales, src):
            nc.vector.quantize_mx(out=codes[:].bitcast(FP8X4), scales=scales[:], in_=src[:])

        def quant_k(b):
            if live(b):
                quantize(k_codes[b % K_BUFS], k_scales[b % K_BUFS], woven[b % 2])

        def quant_q(b, c0=0, c1=COLS):
            quantize(q_codes[b % 2][:, c0:c1], q_scales[b % 2][:, c0:c1], woven[b % 2][:, c0 * PACK : c1 * PACK])

        def quant_p(b, t0=0, t1=PACK):
            cols = slice(t0 * P, t1 * P)
            quantize(p_codes[b % 2][:, cols], p_scales[b % 2][:, cols], p_il[:, t0 * S : t1 * S])

        def quant_v(b):
            if live(b):
                quantize(v_codes[b % 2], v_scales[b % 2], v_il)

        def code_cols(slot, gp):
            at = ((slot // 2) * PASSES + gp) * HALF + (slot % 2) * P
            return slice(at, at + P)

        def scores(b, tq):
            if live(b):
                for tk in range(PACK):
                    for gp in range(PASSES):
                        kc, qc = code_cols(tk, gp), code_cols(tq, gp)
                        nc.tensor.matmul_mx(
                            out=s_bank(b, tq)[:, tk * P : (tk + 1) * P],
                            lhsT=k_codes[b % K_BUFS][:, kc].bitcast(FP8X4),
                            lhsT_scale=k_scales[b % K_BUFS][:, kc],
                            rhs=q_codes[b % 2][:, qc].bitcast(FP8X4),
                            rhs_scale=q_scales[b % 2][:, qc],
                            start=(gp == 0),
                            stop=(gp == PASSES - 1),
                        )

        def relu_root(b, tq):
            if live(b):
                root = g_root[:].rearrange("p (o t) -> p o t", o=1).to_broadcast([P, P, PACK])
                nc.vector.scalar_tensor_tensor(
                    out=r_sb[tq // 2][:, (tq % 2) * S : (tq % 2 + 1) * S].rearrange("p (n t) -> p n t", t=PACK),
                    in0=s_bank(b, tq)[:].rearrange("p (t n) -> p n t", t=PACK),
                    scalar=0.0,
                    in1=root,
                    op0=ALU.max,
                    op1=ALU.mult,
                )

        def square(b, h):
            if live(b):
                nc.scalar.activation(out=p_il[:, h * 2 * S : (h + 1) * 2 * S], in_=r_sb[h][:], func=ACT.Square)

        def square_slot(tq):
            src = r_sb[tq // 2][:, (tq % 2) * S : (tq % 2 + 1) * S]
            nc.scalar.activation(out=p_il[:, tq * S : (tq + 1) * S], in_=src, func=ACT.Square)

        def widen_v(b, planes=range(PACK), on_scalar=False):
            for t in planes:
                cols = slice(t * E, (t + 1) * E)
                dst, src, scale = v_pl[b % 2][:, cols], vb_sb[b % 2][:, cols].bitcast(FP8), vs_signed[:, t : t + 1]
                if on_scalar:
                    nc.scalar.activation(out=dst, in_=src, func=ACT.Copy, scale=scale)
                else:
                    nc.vector.tensor_scalar(out=dst, in0=src, scalar1=scale, scalar2=None, op0=ALU.mult)

        def weave_v(b, bank):
            src = v_pl[b % 2][:].rearrange("p (t e) -> p e t", t=PACK)
            for h in range(2):
                dst = bank[:].bitcast(BF16)[:, h * S : (h + 1) * S].rearrange("p (e t) -> p e t", t=PACK)
                nc.tensor.matmul(out=dst, lhsT=ident16[:], rhs=src[:, h * P : (h + 1) * P, :], start=True, stop=True)

        def fetch_v(bank):
            nc.scalar.copy(out=v_il[:], in_=bank[:].bitcast(BF16))

        def silu(b):
            if live(b):
                nc.scalar.activation(out=gate[b % 2][:], in_=u_sb[b % 2][:], func=ACT.Silu)

        def mix(b, slots=range(PACK)):
            if live(b):
                for tq in slots:
                    cols = slice(tq * P, (tq + 1) * P)
                    nc.tensor.matmul_mx(
                        out=c_place(b, tq),
                        lhsT=p_codes[b % 2][:, cols].bitcast(FP8X4),
                        lhsT_scale=p_scales[b % 2][:, cols],
                        rhs=v_codes[b % 2][:].bitcast(FP8X4),
                        rhs_scale=v_scales[b % 2][:],
                        start=True,
                        stop=True,
                    )

        def finish(b, h):
            if live(b):
                cols = slice(h * 2 * E, (h + 1) * 2 * E)
                nc.vector.tensor_tensor(out=o_sb[b % 2][:, cols], in0=banks[6 + h][:], in1=gate[b % 2][:, cols], op=ALU.mult)

        def finish_slot(b, tq):
            cols = slice(tq * E, (tq + 1) * E)
            nc.vector.tensor_tensor(out=o_sb[b % 2][:, cols], in0=c_place(b, tq), in1=gate[b % 2][:, cols], op=ALU.mult)

        def store(b, h0=0, h1=2):
            if live(b):
                cols = slice(h0 * 2 * E, h1 * 2 * E)
                nc.sync.dma_start(out=out[b].rearrange("(m t) e -> m (t e)", t=PACK)[:, cols], in_=o_sb[b % 2][:, cols])

        ctx.enter_context(tc.manual_schedule())
        load_z(0, range(1))
        load_u(0)
        load_constants()
        load_z(0, range(1, 4))
        nc.sync.dma_start(out=vs_raw[:], in_=v_scale.rearrange("o (p t) x -> p (o t x)", t=PACK))
        load_z(1)
        load_v(0)
        load_z(2)
        make_identity(nc, ident[:])
        nc.vector.tensor_copy(out=ident16[:], in_=ident[:])
        nc.gpsimd.memset(half[:], 0.5)
        widen_gains()
        split_key_gain()
        silu(0)
        for b in range(2):
            for i in range(4):
                turn(b, i)
        make_q(0, 0)
        make_k(0, 1)
        make_q(0, 1)
        make_k(0, 2)
        make_k(0, 0)
        make_q(0, 2)
        make_k(0, 3)
        quant_k(0)
        make_q(0, 3)
        for i in range(4):
            turn(2, i)
        load_z(3)
        make_q(1, 0)
        for h in range(2):
            make_k(1, h + 1)
            make_q(1, h + 1)
            dst, src = weave_q_views(0, h * S, (h + 1) * S)
            nc.vector.tensor_copy(out=dst, in_=src)
            polish_root(h)
        make_k(1, 3)
        make_q(1, 3)
        make_k(1, 0)
        widen_v(0, on_scalar=True)
        quant_q(0)
        polish_root(2)
        scores(0, 0)
        scores(0, 1)
        quant_k(1)
        polish_root(3)

        for n in range(B - 2):
            split = GP_COLS if n >= 1 else GP_COLS_FIRST
            weave_q_gpsimd(n + 1, 0, split)
            load_z(n + 4)
            load_v(n + 1)
            load_u(n + 1)
            dst, src = weave_q_views(n + 1, split, COLS)
            nc.scalar.copy(out=dst, in_=src)
            make_k(n + 2, 0)
            make_q(n + 2, 0)
            make_k(n + 2, 1)
            make_q(n + 2, 1)
            relu_root(n, 0)
            scores(n, 2)
            turn(n + 3, 0)
            make_k(n + 2, 2)
            relu_root(n, 1)
            scores(n, 3)
            turn(n + 3, 1)
            square(n, 0)
            make_k(n + 2, 3)
            relu_root(n, 2)
            finish(n - 1, 0)
            weave_v(n, banks[6])
            relu_root(n, 3)
            finish(n - 1, 1)
            store(n - 1)
            make_q(n + 2, 2)
            turn(n + 3, 2)
            square(n, 1)
            fetch_v(banks[6])
            make_q(n + 2, 3)
            widen_v(n + 1, range(SC_PLANES, PACK))
            quant_q(n + 1)
            scores(n + 1, 0)
            scores(n + 1, 1)
            turn(n + 3, 3)
            quant_p(n)
            quant_k(n + 2)
            quant_v(n)
            mix(n)
            widen_v(n + 1, range(SC_PLANES), on_scalar=True)
            if n >= 1:
                silu(n)

        n = B - 2
        weave_q_gpsimd(n + 1, 0, GP_COLS_LAST)
        load_v(n + 1)
        load_u(n + 1)
        scores(n, 2)
        scores(n, 3)
        dst, src = weave_q_views(n + 1, GP_COLS_LAST, COLS)
        nc.scalar.copy(out=dst, in_=src)
        relu_root(n, 0)
        relu_root(n, 1)
        square(n, 0)
        finish(n - 1, 0)
        weave_v(n, banks[6])
        relu_root(n, 2)
        relu_root(n, 3)
        square(n, 1)
        fetch_v(banks[6])
        finish(n - 1, 1)
        store(n - 1)
        quant_q(n + 1, 0, S)
        scores(n + 1, 0)
        scores(n + 1, 1)
        widen_v(n + 1)
        weave_v(n + 1, banks[0])
        quant_q(n + 1, S, COLS)
        scores(n + 1, 2)
        scores(n + 1, 3)
        silu(n)
        quant_p(n)
        quant_v(n)
        mix(n)
        fetch_v(banks[0])

        n = B - 1
        for tq in range(PACK):
            relu_root(n, tq)
            square_slot(tq)
        silu(n)
        finish(n - 1, 0)
        quant_p(n, 0, 2)
        quant_v(n)
        mix(n, range(2))
        finish(n - 1, 1)
        store(n - 1)
        quant_p(n, 2, 4)
        mix(n, range(2, 4))
        finish_slot(n, 0)
        finish_slot(n, 1)
        store(n, 0, 1)
        finish_slot(n, 2)
        finish_slot(n, 3)
        store(n, 1, 2)
